import numpy as np
import ml_dtypes


def mxq(x, axis, fmt="e4m3"):
    dtype, down = {"e4m3": (ml_dtypes.float8_e4m3fn, 7), "e5m2": (ml_dtypes.float8_e5m2, 14)}[fmt]
    v = np.moveaxis(np.asarray(x, np.float32).astype(ml_dtypes.bfloat16).astype(np.float64), axis, -1)
    blocks = v.reshape(v.shape[:-1] + (-1, 32))
    amax = np.abs(blocks).max(-1, keepdims=True)
    byte = np.maximum(np.where(amax > 0, np.frexp(amax)[1] - 1 + 127, 0) - down, 1)
    scale = np.exp2(byte - 127.0)
    codes = (blocks / scale).astype(np.float32).astype(dtype).astype(np.float64)
    return np.moveaxis((codes * scale).reshape(v.shape), -1, axis)


WIDE = False


def mx_kscale(k):
    if not WIDE:
        return np.ones(k)
    levels = np.array([10, -10, 5, -5, 0])
    if k % 512:
        return np.exp2(np.random.permutation(np.resize(levels, k // 32))).repeat(32)
    a = np.empty((k // 512, 16))
    for p in range(k // 512):
        a[p, :8] = np.random.permutation(np.resize(levels, 8))
        for g in range(8):
            far = levels[np.abs(levels - a[p, g]) >= 10]
            a[p, g + 8] = far[np.random.randint(len(far))]
    return np.exp2(a.ravel()).repeat(32)


def f64(x):
    return np.asarray(x).astype(np.float64)


def striped(idx):
    return np.tile(idx.reshape(-1, 16).T, (8, 1)).astype(np.uint16)


def unstriped(offs):
    return offs[:16].T.reshape(-1).astype(np.int64)


def striped8(idx):
    return np.concatenate([x.reshape(-1, 16).T for x in idx]).astype(np.uint16)


def runs(offs, k):
    lists = np.stack([offs[16 * r : 16 * r + 16].T.reshape(-1) for r in range(8)]).astype(np.int64)
    return lists[np.arange(k) % 512 // 64]


def pack_weight(w):
    k, n = w.shape
    w = f64(np.asarray(w, np.float32).astype(ml_dtypes.bfloat16)).reshape(k // 32, 32, n)
    amax = np.abs(w).max(1)
    byte = np.clip(np.where(amax > 0, np.frexp(amax)[1] - 1 + 127 - 7, 1), 1, 254)
    scaled = (w * np.exp2(127.0 - byte)[:, None, :]).reshape(k, n).astype(np.float32)
    words = np.ascontiguousarray(scaled.reshape(k // 512, 128, 4, n).transpose(0, 1, 3, 2)).astype(ml_dtypes.float8_e4m3fn).view(np.uint8)
    return words, np.ascontiguousarray(byte.astype(np.uint8).reshape(k // 512, 16, n))


def unpack_weight(words, scales):
    g, p, n, _ = words.shape
    vals = np.ascontiguousarray(words).view(ml_dtypes.float8_e4m3fn).astype(np.float64) * np.repeat(np.exp2(scales.astype(np.float64) - 127.0), 8, axis=1)[..., None]
    return vals.transpose(0, 1, 3, 2).reshape(g * 512, n)


def sigmoid(v):
    return 1.0 / (1.0 + np.exp(-np.maximum(v, -700.0)))


K, T, S, N, H, W = 512, 2048, 512, 512, 512, 256


def setup_inputs():
    n = np.random.standard_normal
    s = mx_kscale(K)[:, None]
    u = mx_kscale(H)
    packed_xT = pack_weight(n((K, T)) * s)
    perm = np.stack([np.random.permutation(S) for _ in range(8)])
    return {
        "x_words": packed_xT[0],
        "x_scales": packed_xT[1],
        "w1": (n((K, H)) / np.sqrt(K) / s).astype(np.float32),
        "gn": (np.random.uniform(0.5, 1.5, (H, 1)) * u[:, None]).astype(np.float32),
        "w2": (n((H, N)) / np.sqrt(H) / u[:, None]).astype(np.float32),
        "offs": striped(np.random.permutation(T)[:S]),
        "n1": striped8(np.stack([np.random.permutation(S) for _ in range(8)])),
        "n2": striped8(perm[:, :W]),
        "n3": striped8(perm[:, W:]),
    }


def reference(x_words, x_scales, w1, gn, w2, offs, n1, n2, n3):
    xq = unpack_weight(x_words, x_scales)[:, unstriped(offs)]
    y = mxq(f64(w1), 0, "e4m3").T @ xq
    st = y - (y[np.arange(H)[:, None], runs(n1, H)])
    z = f64(gn) * (st - (0.5 * (st[np.arange(H)[:, None], runs(n1, H)])))
    h = mxq(f64(w2), 0, "e4m3").T @ mxq(z, 0, "e4m3")
    pa = h[np.arange(N)[:, None], runs(n2, N)]
    pb = h[np.arange(N)[:, None], runs(n3, N)]
    ra = pa * sigmoid(pb)
    out = h.copy()
    out[np.arange(N)[:, None], runs(n3, N)] = ra
    return out

@@ -1,0 +1,192 @@
+from contextlib import ExitStack
+
+import concourse.mybir as mybir
+
+K, T, S, H, N, W = 512, 2048, 512, 512, 512, 256
+FLOPS = 2 * K * H * S + 2 * H * N * S
+
+F32 = mybir.dt.float32
+BF16 = mybir.dt.bfloat16
+I32 = mybir.dt.int32
+U32 = mybir.dt.uint32
+U16 = mybir.dt.uint16
+U8 = mybir.dt.uint8
+FP8X4 = mybir.dt.float8_e4m3fn_x4
+MULT = mybir.AluOpType.mult
+SUB = mybir.AluOpType.subtract
+COPY = mybir.ActivationFunctionType.Copy
+SIGMOID = mybir.ActivationFunctionType.Sigmoid
+
+P = 128
+PACK = 4
+HALF = S // 2
+CHUNKS = ((0, 256), (256, 384), (384, 512))
+
+
+def tile_picked_laytwicefold_none_p_kernel(tc, x_words, x_scales, w1, gn, w2, offs, n1, n2, n3, out):
+    nc = tc.nc
+    with ExitStack() as ctx:
+        lists = ctx.enter_context(tc.tile_pool(name="lists", bufs=1))
+        keep = ctx.enter_context(tc.tile_pool(name="keep", bufs=1))
+        psum = ctx.enter_context(tc.psum_pool(name="psum", bufs=1))
+
+        offs_t = lists.tile([P, S // 16], U16, name="offs_t")
+        n1_t = lists.tile([P, S // 16], U16, name="n1_t")
+        n2_t = lists.tile([P, W // 16], U16, name="n2_t")
+        n3_t = lists.tile([P, W // 16], U16, name="n3_t")
+
+        def cols16(lo, hi):
+            return slice(lo // 16, hi // 16)
+
+        xw = keep.tile([P, T], U32, name="xw")
+        xs = keep.tile([P, T], U8, name="xs")
+        w1_raw = keep.tile([P, PACK, H], F32, name="w1_raw")
+        w2_raw = keep.tile([P, PACK, N], F32, name="w2_raw")
+        gain = keep.tile([P, PACK], F32, name="gain")
+
+        nc.vector.memset(xs[:].bitcast(I32), 0)
+        nc.sync.dma_start(offs_t[:], offs)
+        nc.sync.dma_start(w1_raw[:], w1.rearrange("(p j) c -> p j c", j=PACK))
+        for q in range(4):
+            nc.scalar.dma_start(xs[32 * q : 32 * q + 4, :].bitcast(I32), x_scales[0, 4 * q : 4 * q + 4, :].bitcast(I32))
+        nc.sync.dma_start(xw[:].bitcast(I32), x_words[0].rearrange("p c r -> p (c r)").bitcast(I32))
+        nc.sync.dma_start(gain[:], gn.rearrange("(p t) o -> p (t o)", t=PACK))
+        nc.sync.dma_start(n1_t[:], n1)
+        nc.sync.dma_start(w2_raw[:], w2.rearrange("(p j) c -> p j c", j=PACK))
+        nc.sync.dma_start(n2_t[:], n2)
+        nc.sync.dma_start(n3_t[:], n3)
+
+        warm_in = keep.tile([P, 1], F32, name="warm_in")
+        warm_out = keep.tile([P, 1], F32, name="warm_out")
+        nc.vector.memset(warm_in[:], 0.0)
+        nc.scalar.activation(warm_out[:], warm_in[:], SIGMOID)
+
+        def weight_pair(name):
+            grouped = keep.tile([P, 2 * P * PACK], BF16, name=name + "_bf", align_bytes=64)
+            codes = keep.tile([P, 2 * P], U32, name=name + "_codes", align_bytes=64)
+            scales = keep.tile([P, 2 * P], U8, name=name + "_scales", align_bytes=64)
+            return grouped, codes, scales
+
+        def cast_pair(copy, raw, pair, grouped):
+            copy(
+                grouped[:].rearrange("p (t m j) -> p m j t", t=2, j=PACK),
+                raw[:].rearrange("p j (m t) -> p m j t", t=PACK)[:, :, :, 2 * pair : 2 * pair + 2],
+            )
+
+        def quantize(grouped, codes, scales):
+            nc.vector.quantize_mx(out=codes.bitcast(FP8X4), scales=scales, in_=grouped)
+
+        def product(acc, wq, t, codes, scales):
+            m = slice((t % 2) * P, (t % 2 + 1) * P)
+            nc.tensor.matmul_mx(
+                out=acc,
+                lhsT=wq[t // 2][1][:, m].bitcast(FP8X4),
+                lhsT_scale=wq[t // 2][2][:, m],
+                rhs=codes.bitcast(FP8X4),
+                rhs_scale=scales,
+                start=True,
+                stop=True,
+            )
+
+        w1q = [weight_pair("w1a"), weight_pair("w1b")]
+        w2q = [weight_pair("w2a"), weight_pair("w2b")]
+
+        xg = keep.tile([P, S], U32, name="xg", align_bytes=64)
+        sg = keep.tile([P, S], U8, name="sg", align_bytes=64)
+        nc.vector.tensor_copy(sg[:], xs[:].indirect(offs_t[:]))
+        cast_pair(nc.vector.tensor_copy, w1_raw, 0, w1q[0][0])
+        cast_pair(nc.scalar.copy, w1_raw, 1, w1q[1][0])
+        gain_half = keep.tile([P, PACK], F32, name="gain_half")
+        nc.vector.tensor_scalar(gain_half[:], gain[:], 0.5, None, MULT)
+        for g in w1q:
+            quantize(g[0][:], g[1][:], g[2][:])
+
+        halves = (slice(0, HALF), slice(HALF, S))
+        for c in halves:
+            nc.vector.tensor_copy(xg[:, c], xw[:].indirect(offs_t[:, cols16(c.start, c.stop)]))
+
+        y0 = [psum.tile([P, HALF], F32, name="y0_%d" % i) for i in range(2)]
+        yb = [None] + [psum.tile([P, S], F32, name="y%d" % t, tag="bank%d" % t) for t in range(1, PACK)]
+        for i, c in enumerate(halves):
+            product(y0[i][:], w1q, 0, xg[:, c], sg[:, c])
+        for t in range(1, PACK):
+            product(yb[t][:], w1q, t, xg[:], sg[:])
+
+        a_half = [keep.tile([P, S], F32, name="a_half%d" % t) for t in range(PACK)]
+        a_more = [keep.tile([P, S], F32, name="a_more%d" % t) for t in range(PACK)]
+        a_full = [keep.tile([P, S], F32, name="a_full%d" % t) for t in range(PACK)]
+        u = [keep.tile([P, S], F32, name="u%d" % t) for t in range(PACK)]
+
+        def scaled(dst, t, factor):
+            if t == 0:
+                for i, c in enumerate(halves):
+                    nc.scalar.activation(dst[:, c], y0[i][:], COPY, scale=factor[:, 0:1])
+            else:
+                nc.scalar.activation(dst[:], yb[t][:], COPY, scale=factor[:, t : t + 1])
+
+        def first_lookup(t):
+            for c in halves:
+                nc.vector.tensor_tensor(u[t][:, c], a_half[t][:].indirect(n1_t[:, cols16(c.start, c.stop)]), a_more[t][:, c], SUB)
+
+        scaled(a_half[0], 0, gain_half)
+        nc.vector.tensor_scalar(a_more[0][:, halves[0]], y0[0][:], gain_half[:, 0:1], None, MULT)
+        nc.scalar.activation(a_more[0][:, halves[1]], y0[1][:], COPY, scale=gain_half[:, 0:1])
+        first_lookup(0)
+        for t in range(1, PACK):
+            scaled(a_half[t], t, gain_half)
+            scaled(a_more[t], t, gain_half)
+            first_lookup(t)
+        for t in range(PACK):
+            nc.scalar.activation(a_full[t][:], u[t][:], COPY, scale=2.0)
+
+        z32 = [keep.tile([P, PACK, hi - lo], F32, name="z32_%d" % i) for i, (lo, hi) in enumerate(CHUNKS)]
+        z16 = [keep.tile([P, PACK * (hi - lo)], BF16, name="z16_%d" % i, align_bytes=64) for i, (lo, hi) in enumerate(CHUNKS)]
+        zq = keep.tile([P, S], U32, name="zq", align_bytes=64)
+        zs = keep.tile([P, S], U8, name="zs", align_bytes=64)
+        h0 = [psum.tile([P, hi - lo], F32, name="h0_%d" % i) for i, (lo, hi) in enumerate(CHUNKS)]
+        h = [keep.tile([P, S], F32, name="h%d" % t) for t in range(PACK)]
+
+        def second_lookup(i):
+            lo, hi = CHUNKS[i]
+            for t in range(PACK):
+                nc.vector.tensor_tensor(z32[i][:, t, :], u[t][:].indirect(n1_t[:, cols16(lo, hi)]), a_full[t][:, lo:hi], SUB)
+
+        def weave(copy, i):
+            copy(
+                z16[i][:].rearrange("p (c e t) -> p c t e", e=4, t=PACK),
+                z32[i][:].rearrange("p t (c e) -> p c t e", e=4),
+            )
+
+        def finish_chunk(i):
+            lo, hi = CHUNKS[i]
+            quantize(z16[i][:], zq[:, lo:hi], zs[:, lo:hi])
+            product(h0[i][:], w2q, 0, zq[:, lo:hi], zs[:, lo:hi])
+            nc.scalar.copy(h[0][:, lo:hi], h0[i][:])
+
+        second_lookup(0)
+        cast_pair(nc.scalar.copy, w2_raw, 0, w2q[0][0])
+        weave(nc.scalar.copy, 0)
+        second_lookup(1)
+        quantize(w2q[0][0][:], w2q[0][1][:], w2q[0][2][:])
+        weave(nc.scalar.copy, 1)
+        finish_chunk(0)
+        second_lookup(2)
+        weave(nc.vector.tensor_copy, 2)
+        finish_chunk(1)
+        finish_chunk(2)
+
+        out_rows = out.rearrange("(p t) n -> p t n", t=PACK)
+        for t in range(PACK):
+            if t > 0:
+                hb = psum.tile([P, S], F32, name="hb%d" % t, tag="bank%d" % t)
+                product(hb[:], w2q, t, zq[:], zs[:])
+                nc.scalar.copy(h[t][:], hb[:])
+            gate = keep.tile([P, W], F32, name="gate%d" % t)
+            pa = keep.tile([P, W], F32, name="pa%d" % t)
+            nc.scalar.activation(gate[:], h[t][:].indirect(n3_t[:]), SIGMOID)
+            nc.vector.tensor_copy(pa[:], h[t][:].indirect(n2_t[:]))
+            nc.vector.tensor_tensor(h[t][:].indirect(n3_t[:]), pa[:], gate[:], MULT)
+            nc.sync.dma_start(out_rows[:, t, :], h[t][:])
+            if t == 0:
+                cast_pair(nc.scalar.copy, w2_raw, 1, w2q[1][0])
+                quantize(w2q[1][0][:], w2q[1][1][:], w2q[1][2][:])

@@ -46,9 +46,10 @@ def tile_picked_laytwicefold_none_p_kernel(tc, x_words, x_scales, w1, gn, w2, of
 
         nc.vector.memset(xs[:].bitcast(I32), 0)
         nc.sync.dma_start(offs_t[:], offs)
-        nc.sync.dma_start(w1_raw[:], w1.rearrange("(p j) c -> p j c", j=PACK))
+        xs_in = keep.tile([P, T // 4], I32, name="xs_in")
         for q in range(4):
-            nc.scalar.dma_start(xs[32 * q : 32 * q + 4, :].bitcast(I32), x_scales[0, 4 * q : 4 * q + 4, :].bitcast(I32))
+            (nc.sync if q < 2 else nc.scalar).dma_start(xs_in[32 * q : 32 * q + 4, :], x_scales[0, 4 * q : 4 * q + 4, :].bitcast(I32))
+        nc.sync.dma_start(w1_raw[:], w1.rearrange("(p j) c -> p j c", j=PACK))
         nc.sync.dma_start(xw[:].bitcast(I32), x_words[0].rearrange("p c r -> p (c r)").bitcast(I32))
         nc.sync.dma_start(gain[:], gn.rearrange("(p t) o -> p (t o)", t=PACK))
         nc.sync.dma_start(n1_t[:], n1)
@@ -61,8 +62,8 @@ def tile_picked_laytwicefold_none_p_kernel(tc, x_words, x_scales, w1, gn, w2, of
         nc.vector.memset(warm_in[:], 0.0)
         nc.scalar.activation(warm_out[:], warm_in[:], SIGMOID)
 
-        def weight_pair(name):
-            grouped = keep.tile([P, 2 * P * PACK], BF16, name=name + "_bf", align_bytes=64)
+        def weight_pair(name, tag):
+            grouped = keep.tile([P, 2 * P * PACK], BF16, name=name + "_bf", tag=tag, align_bytes=64)
             codes = keep.tile([P, 2 * P], U32, name=name + "_codes", align_bytes=64)
             scales = keep.tile([P, 2 * P], U8, name=name + "_scales", align_bytes=64)
             return grouped, codes, scales
@@ -88,16 +89,17 @@ def tile_picked_laytwicefold_none_p_kernel(tc, x_words, x_scales, w1, gn, w2, of
                 stop=True,
             )
 
-        w1q = [weight_pair("w1a"), weight_pair("w1b")]
-        w2q = [weight_pair("w2a"), weight_pair("w2b")]
+        w1q = [weight_pair("w1a", "w1a_bf"), weight_pair("w1b", "w1b_bf")]
+        w2q = [weight_pair("w2a", "w2a_bf"), weight_pair("w2b", "w2b_bf")]
 
         xg = keep.tile([P, S], U32, name="xg", align_bytes=64)
         sg = keep.tile([P, S], U8, name="sg", align_bytes=64)
+        for q in range(4):
+            nc.vector.tensor_copy(xs[32 * q : 32 * q + 4, :].bitcast(I32), xs_in[32 * q : 32 * q + 4, :])
         nc.vector.tensor_copy(sg[:], xs[:].indirect(offs_t[:]))
         cast_pair(nc.vector.tensor_copy, w1_raw, 0, w1q[0][0])
         cast_pair(nc.scalar.copy, w1_raw, 1, w1q[1][0])
         gain_half = keep.tile([P, PACK], F32, name="gain_half")
-        nc.vector.tensor_scalar(gain_half[:], gain[:], 0.5, None, MULT)
         for g in w1q:
             quantize(g[0][:], g[1][:], g[2][:])
 
@@ -105,6 +107,7 @@ def tile_picked_laytwicefold_none_p_kernel(tc, x_words, x_scales, w1, gn, w2, of
         for c in halves:
             nc.vector.tensor_copy(xg[:, c], xw[:].indirect(offs_t[:, cols16(c.start, c.stop)]))
 
+        nc.vector.tensor_scalar(gain_half[:], gain[:], 0.5, None, MULT)
         y0 = [psum.tile([P, HALF], F32, name="y0_%d" % i) for i in range(2)]
         yb = [None] + [psum.tile([P, S], F32, name="y%d" % t, tag="bank%d" % t) for t in range(1, PACK)]
         for i, c in enumerate(halves):
@@ -112,8 +115,10 @@ def tile_picked_laytwicefold_none_p_kernel(tc, x_words, x_scales, w1, gn, w2, of
         for t in range(1, PACK):
             product(yb[t][:], w1q, t, xg[:], sg[:])
 
-        a_half = [keep.tile([P, S], F32, name="a_half%d" % t) for t in range(PACK)]
-        a_more = [keep.tile([P, S], F32, name="a_more%d" % t) for t in range(PACK)]
+        window = [keep.tile([P, S if t == 0 else 2 * S], F32, name="window%d" % t) for t in range(PACK)]
+        last_more = keep.tile([P, S], F32, name="last_more")
+        a_half = [w[:, 0:S] for w in window]
+        a_more = [w[:, S : 2 * S] for w in window[1:]] + [last_more[:]]
         a_full = [keep.tile([P, S], F32, name="a_full%d" % t) for t in range(PACK)]
         u = [keep.tile([P, S], F32, name="u%d" % t) for t in range(PACK)]
 
@@ -122,11 +127,11 @@ def tile_picked_laytwicefold_none_p_kernel(tc, x_words, x_scales, w1, gn, w2, of
                 for i, c in enumerate(halves):
                     nc.scalar.activation(dst[:, c], y0[i][:], COPY, scale=factor[:, 0:1])
             else:
-                nc.scalar.activation(dst[:], yb[t][:], COPY, scale=factor[:, t : t + 1])
+                nc.scalar.activation(dst, yb[t][:], COPY, scale=factor[:, t : t + 1])
 
         def first_lookup(t):
-            for c in halves:
-                nc.vector.tensor_tensor(u[t][:, c], a_half[t][:].indirect(n1_t[:, cols16(c.start, c.stop)]), a_more[t][:, c], SUB)
+            for c in halves if t == 0 else [slice(0, S)]:
+                nc.vector.tensor_tensor(u[t][:, c], window[t][:].indirect(n1_t[:, cols16(c.start, c.stop)]), a_more[t][:, c], SUB)
 
         scaled(a_half[0], 0, gain_half)
         nc.vector.tensor_scalar(a_more[0][:, halves[0]], y0[0][:], gain_half[:, 0:1], None, MULT)
@@ -136,11 +141,9 @@ def tile_picked_laytwicefold_none_p_kernel(tc, x_words, x_scales, w1, gn, w2, of
             scaled(a_half[t], t, gain_half)
             scaled(a_more[t], t, gain_half)
             first_lookup(t)
-        for t in range(PACK):
-            nc.scalar.activation(a_full[t][:], u[t][:], COPY, scale=2.0)
 
         z32 = [keep.tile([P, PACK, hi - lo], F32, name="z32_%d" % i) for i, (lo, hi) in enumerate(CHUNKS)]
-        z16 = [keep.tile([P, PACK * (hi - lo)], BF16, name="z16_%d" % i, align_bytes=64) for i, (lo, hi) in enumerate(CHUNKS)]
+        z16 = [keep.tile([P, PACK * (hi - lo)], BF16, name="z16_%d" % i, tag="z16_%d" % i, align_bytes=64) for i, (lo, hi) in enumerate(CHUNKS)]
         zq = keep.tile([P, S], U32, name="zq", align_bytes=64)
         zs = keep.tile([P, S], U8, name="zs", align_bytes=64)
         h0 = [psum.tile([P, hi - lo], F32, name="h0_%d" % i) for i, (lo, hi) in enumerate(CHUNKS)]
@@ -148,6 +151,8 @@ def tile_picked_laytwicefold_none_p_kernel(tc, x_words, x_scales, w1, gn, w2, of
 
         def second_lookup(i):
             lo, hi = CHUNKS[i]
+            for t in range(PACK):
+                nc.scalar.activation(a_full[t][:, lo:hi], u[t][:, lo:hi], COPY, scale=2.0)
             for t in range(PACK):
                 nc.vector.tensor_tensor(z32[i][:, t, :], u[t][:].indirect(n1_t[:, cols16(lo, hi)]), a_full[t][:, lo:hi], SUB)
 
@@ -157,23 +162,29 @@ def tile_picked_laytwicefold_none_p_kernel(tc, x_words, x_scales, w1, gn, w2, of
                 z32[i][:].rearrange("p t (c e) -> p c t e", e=4),
             )
 
-        def finish_chunk(i):
+        def quantize_chunk(i):
             lo, hi = CHUNKS[i]
             quantize(z16[i][:], zq[:, lo:hi], zs[:, lo:hi])
+
+        def finish_chunk(i):
+            lo, hi = CHUNKS[i]
             product(h0[i][:], w2q, 0, zq[:, lo:hi], zs[:, lo:hi])
             nc.scalar.copy(h[0][:, lo:hi], h0[i][:])
 
         second_lookup(0)
+        second_lookup(1)
         cast_pair(nc.scalar.copy, w2_raw, 0, w2q[0][0])
         weave(nc.scalar.copy, 0)
-        second_lookup(1)
         quantize(w2q[0][0][:], w2q[0][1][:], w2q[0][2][:])
-        weave(nc.scalar.copy, 1)
-        finish_chunk(0)
+        quantize_chunk(0)
         second_lookup(2)
+        weave(nc.scalar.copy, 1)
+        cast_pair(nc.scalar.copy, w2_raw, 1, w2q[1][0])
         weave(nc.vector.tensor_copy, 2)
-        finish_chunk(1)
-        finish_chunk(2)
+        quantize_chunk(1)
+        quantize_chunk(2)
+        for i in range(len(CHUNKS)):
+            finish_chunk(i)
 
         out_rows = out.rearrange("(p t) n -> p t n", t=PACK)
         for t in range(PACK):
@@ -188,5 +199,4 @@ def tile_picked_laytwicefold_none_p_kernel(tc, x_words, x_scales, w1, gn, w2, of
             nc.vector.tensor_tensor(h[t][:].indirect(n3_t[:]), pa[:], gate[:], MULT)
             nc.sync.dma_start(out_rows[:, t, :], h[t][:])
             if t == 0:
-                cast_pair(nc.scalar.copy, w2_raw, 1, w2q[1][0])
                 quantize(w2q[1][0][:], w2q[1][1][:], w2q[1][2][:])

@@ -187,16 +187,21 @@ def tile_picked_laytwicefold_none_p_kernel(tc, x_words, x_scales, w1, gn, w2, of
             finish_chunk(i)
 
         out_rows = out.rearrange("(p t) n -> p t n", t=PACK)
-        for t in range(PACK):
+        gate = [keep.tile([P, W], F32, name="gate%d" % t) for t in range(PACK)]
+        pa = [keep.tile([P, W], F32, name="pa%d" % t) for t in range(PACK)]
+
+        def fetch(t):
             if t > 0:
                 hb = psum.tile([P, S], F32, name="hb%d" % t, tag="bank%d" % t)
                 product(hb[:], w2q, t, zq[:], zs[:])
                 nc.scalar.copy(h[t][:], hb[:])
-            gate = keep.tile([P, W], F32, name="gate%d" % t)
-            pa = keep.tile([P, W], F32, name="pa%d" % t)
-            nc.scalar.activation(gate[:], h[t][:].indirect(n3_t[:]), SIGMOID)
-            nc.vector.tensor_copy(pa[:], h[t][:].indirect(n2_t[:]))
-            nc.vector.tensor_tensor(h[t][:].indirect(n3_t[:]), pa[:], gate[:], MULT)
+            nc.vector.tensor_copy(pa[t][:], h[t][:].indirect(n2_t[:]))
+
+        fetch(0)
+        quantize(w2q[1][0][:], w2q[1][1][:], w2q[1][2][:])
+        for t in range(PACK):
+            if t + 1 < PACK:
+                fetch(t + 1)
+            nc.scalar.activation(gate[t][:], h[t][:].indirect(n3_t[:]), SIGMOID)
+            nc.vector.tensor_tensor(h[t][:].indirect(n3_t[:]), pa[t][:], gate[t][:], MULT)
             nc.sync.dma_start(out_rows[:, t, :], h[t][:])
-            if t == 0:
-                quantize(w2q[1][0][:], w2q[1][1][:], w2q[1][2][:])

from contextlib import ExitStack

import concourse.mybir as mybir

K, T, S, H, N, W = 512, 2048, 512, 512, 512, 256
FLOPS = 2 * K * H * S + 2 * H * N * S

F32 = mybir.dt.float32
BF16 = mybir.dt.bfloat16
I32 = mybir.dt.int32
U32 = mybir.dt.uint32
U16 = mybir.dt.uint16
U8 = mybir.dt.uint8
FP8X4 = mybir.dt.float8_e4m3fn_x4
MULT = mybir.AluOpType.mult
SUB = mybir.AluOpType.subtract
COPY = mybir.ActivationFunctionType.Copy
SIGMOID = mybir.ActivationFunctionType.Sigmoid

P = 128
PACK = 4
HALF = S // 2
CHUNKS = ((0, 256), (256, 384), (384, 512))


def tile_picked_laytwicefold_none_p_kernel(tc, x_words, x_scales, w1, gn, w2, offs, n1, n2, n3, out):
    nc = tc.nc
    with ExitStack() as ctx:
        lists = ctx.enter_context(tc.tile_pool(name="lists", bufs=1))
        keep = ctx.enter_context(tc.tile_pool(name="keep", bufs=1))
        psum = ctx.enter_context(tc.psum_pool(name="psum", bufs=1))

        offs_t = lists.tile([P, S // 16], U16, name="offs_t")
        n1_t = lists.tile([P, S // 16], U16, name="n1_t")
        n2_t = lists.tile([P, W // 16], U16, name="n2_t")
        n3_t = lists.tile([P, W // 16], U16, name="n3_t")

        def cols16(lo, hi):
            return slice(lo // 16, hi // 16)

        xw = keep.tile([P, T], U32, name="xw")
        xs = keep.tile([P, T], U8, name="xs")
        w1_raw = keep.tile([P, PACK, H], F32, name="w1_raw")
        w2_raw = keep.tile([P, PACK, N], F32, name="w2_raw")
        gain = keep.tile([P, PACK], F32, name="gain")

        nc.vector.memset(xs[:].bitcast(I32), 0)
        nc.sync.dma_start(offs_t[:], offs)
        xs_in = keep.tile([P, T // 4], I32, name="xs_in")
        for q in range(4):
            (nc.sync if q < 2 else nc.scalar).dma_start(xs_in[32 * q : 32 * q + 4, :], x_scales[0, 4 * q : 4 * q + 4, :].bitcast(I32))
        nc.sync.dma_start(w1_raw[:], w1.rearrange("(p j) c -> p j c", j=PACK))
        nc.sync.dma_start(xw[:].bitcast(I32), x_words[0].rearrange("p c r -> p (c r)").bitcast(I32))
        nc.sync.dma_start(gain[:], gn.rearrange("(p t) o -> p (t o)", t=PACK))
        nc.sync.dma_start(n1_t[:], n1)
        nc.sync.dma_start(w2_raw[:], w2.rearrange("(p j) c -> p j c", j=PACK))
        nc.sync.dma_start(n2_t[:], n2)
        nc.sync.dma_start(n3_t[:], n3)

        warm_in = keep.tile([P, 1], F32, name="warm_in")
        warm_out = keep.tile([P, 1], F32, name="warm_out")
        nc.vector.memset(warm_in[:], 0.0)
        nc.scalar.activation(warm_out[:], warm_in[:], SIGMOID)

        def weight_pair(name, tag):
            grouped = keep.tile([P, 2 * P * PACK], BF16, name=name + "_bf", tag=tag, align_bytes=64)
            codes = keep.tile([P, 2 * P], U32, name=name + "_codes", align_bytes=64)
            scales = keep.tile([P, 2 * P], U8, name=name + "_scales", align_bytes=64)
            return grouped, codes, scales

        def cast_pair(copy, raw, pair, grouped):
            copy(
                grouped[:].rearrange("p (t m j) -> p m j t", t=2, j=PACK),
                raw[:].rearrange("p j (m t) -> p m j t", t=PACK)[:, :, :, 2 * pair : 2 * pair + 2],
            )

        def quantize(grouped, codes, scales):
            nc.vector.quantize_mx(out=codes.bitcast(FP8X4), scales=scales, in_=grouped)

        def product(acc, wq, t, codes, scales):
            m = slice((t % 2) * P, (t % 2 + 1) * P)
            nc.tensor.matmul_mx(
                out=acc,
                lhsT=wq[t // 2][1][:, m].bitcast(FP8X4),
                lhsT_scale=wq[t // 2][2][:, m],
                rhs=codes.bitcast(FP8X4),
                rhs_scale=scales,
                start=True,
                stop=True,
            )

        w1q = [weight_pair("w1a", "w1a_bf"), weight_pair("w1b", "w1b_bf")]
        w2q = [weight_pair("w2a", "w2a_bf"), weight_pair("w2b", "w2b_bf")]

        xg = keep.tile([P, S], U32, name="xg", align_bytes=64)
        sg = keep.tile([P, S], U8, name="sg", align_bytes=64)
        for q in range(4):
            nc.vector.tensor_copy(xs[32 * q : 32 * q + 4, :].bitcast(I32), xs_in[32 * q : 32 * q + 4, :])
        nc.vector.tensor_copy(sg[:], xs[:].indirect(offs_t[:]))
        cast_pair(nc.vector.tensor_copy, w1_raw, 0, w1q[0][0])
        cast_pair(nc.scalar.copy, w1_raw, 1, w1q[1][0])
        gain_half = keep.tile([P, PACK], F32, name="gain_half")
        for g in w1q:
            quantize(g[0][:], g[1][:], g[2][:])

        halves = (slice(0, HALF), slice(HALF, S))
        for c in halves:
            nc.vector.tensor_copy(xg[:, c], xw[:].indirect(offs_t[:, cols16(c.start, c.stop)]))

        nc.vector.tensor_scalar(gain_half[:], gain[:], 0.5, None, MULT)
        y0 = [psum.tile([P, HALF], F32, name="y0_%d" % i) for i in range(2)]
        yb = [None] + [psum.tile([P, S], F32, name="y%d" % t, tag="bank%d" % t) for t in range(1, PACK)]
        for i, c in enumerate(halves):
            product(y0[i][:], w1q, 0, xg[:, c], sg[:, c])
        for t in range(1, PACK):
            product(yb[t][:], w1q, t, xg[:], sg[:])

        window = [keep.tile([P, S if t == 0 else 2 * S], F32, name="window%d" % t) for t in range(PACK)]
        last_more = keep.tile([P, S], F32, name="last_more")
        a_half = [w[:, 0:S] for w in window]
        a_more = [w[:, S : 2 * S] for w in window[1:]] + [last_more[:]]
        a_full = [keep.tile([P, S], F32, name="a_full%d" % t) for t in range(PACK)]
        u = [keep.tile([P, S], F32, name="u%d" % t) for t in range(PACK)]

        def scaled(dst, t, factor):
            if t == 0:
                for i, c in enumerate(halves):
                    nc.scalar.activation(dst[:, c], y0[i][:], COPY, scale=factor[:, 0:1])
            else:
                nc.scalar.activation(dst, yb[t][:], COPY, scale=factor[:, t : t + 1])

        def first_lookup(t):
            for c in halves if t == 0 else [slice(0, S)]:
                nc.vector.tensor_tensor(u[t][:, c], window[t][:].indirect(n1_t[:, cols16(c.start, c.stop)]), a_more[t][:, c], SUB)

        scaled(a_half[0], 0, gain_half)
        nc.vector.tensor_scalar(a_more[0][:, halves[0]], y0[0][:], gain_half[:, 0:1], None, MULT)
        nc.scalar.activation(a_more[0][:, halves[1]], y0[1][:], COPY, scale=gain_half[:, 0:1])
        first_lookup(0)
        for t in range(1, PACK):
            scaled(a_half[t], t, gain_half)
            scaled(a_more[t], t, gain_half)
            first_lookup(t)

        z32 = [keep.tile([P, PACK, hi - lo], F32, name="z32_%d" % i) for i, (lo, hi) in enumerate(CHUNKS)]
        z16 = [keep.tile([P, PACK * (hi - lo)], BF16, name="z16_%d" % i, tag="z16_%d" % i, align_bytes=64) for i, (lo, hi) in enumerate(CHUNKS)]
        zq = keep.tile([P, S], U32, name="zq", align_bytes=64)
        zs = keep.tile([P, S], U8, name="zs", align_bytes=64)
        h0 = [psum.tile([P, hi - lo], F32, name="h0_%d" % i) for i, (lo, hi) in enumerate(CHUNKS)]
        h = [keep.tile([P, S], F32, name="h%d" % t) for t in range(PACK)]

        def second_lookup(i):
            lo, hi = CHUNKS[i]
            for t in range(PACK):
                nc.scalar.activation(a_full[t][:, lo:hi], u[t][:, lo:hi], COPY, scale=2.0)
            for t in range(PACK):
                nc.vector.tensor_tensor(z32[i][:, t, :], u[t][:].indirect(n1_t[:, cols16(lo, hi)]), a_full[t][:, lo:hi], SUB)

        def weave(copy, i):
            copy(
                z16[i][:].rearrange("p (c e t) -> p c t e", e=4, t=PACK),
                z32[i][:].rearrange("p t (c e) -> p c t e", e=4),
            )

        def quantize_chunk(i):
            lo, hi = CHUNKS[i]
            quantize(z16[i][:], zq[:, lo:hi], zs[:, lo:hi])

        def finish_chunk(i):
            lo, hi = CHUNKS[i]
            product(h0[i][:], w2q, 0, zq[:, lo:hi], zs[:, lo:hi])
            nc.scalar.copy(h[0][:, lo:hi], h0[i][:])

        second_lookup(0)
        second_lookup(1)
        cast_pair(nc.scalar.copy, w2_raw, 0, w2q[0][0])
        weave(nc.scalar.copy, 0)
        quantize(w2q[0][0][:], w2q[0][1][:], w2q[0][2][:])
        quantize_chunk(0)
        second_lookup(2)
        weave(nc.scalar.copy, 1)
        cast_pair(nc.scalar.copy, w2_raw, 1, w2q[1][0])
        weave(nc.vector.tensor_copy, 2)
        quantize_chunk(1)
        quantize_chunk(2)
        for i in range(len(CHUNKS)):
            finish_chunk(i)

        out_rows = out.rearrange("(p t) n -> p t n", t=PACK)
        gate = [keep.tile([P, W], F32, name="gate%d" % t) for t in range(PACK)]
        pa = [keep.tile([P, W], F32, name="pa%d" % t) for t in range(PACK)]

        def fetch(t):
            if t > 0:
                hb = psum.tile([P, S], F32, name="hb%d" % t, tag="bank%d" % t)
                product(hb[:], w2q, t, zq[:], zs[:])
                nc.scalar.copy(h[t][:], hb[:])
            nc.vector.tensor_copy(pa[t][:], h[t][:].indirect(n2_t[:]))

        fetch(0)
        quantize(w2q[1][0][:], w2q[1][1][:], w2q[1][2][:])
        for t in range(PACK):
            if t + 1 < PACK:
                fetch(t + 1)
            nc.scalar.activation(gate[t][:], h[t][:].indirect(n3_t[:]), SIGMOID)
            nc.vector.tensor_tensor(h[t][:].indirect(n3_t[:]), pa[t][:], gate[t][:], MULT)
            nc.sync.dma_start(out_rows[:, t, :], h[t][:])
